import numpy as np
import ml_dtypes


def mxq(x, axis, fmt="e4m3"):
    dtype, down = {"e4m3": (ml_dtypes.float8_e4m3fn, 7), "e5m2": (ml_dtypes.float8_e5m2, 14)}[fmt]
    v = np.moveaxis(np.asarray(x, np.float32).astype(ml_dtypes.bfloat16).astype(np.float64), axis, -1)
    blocks = v.reshape(v.shape[:-1] + (-1, 32))
    amax = np.abs(blocks).max(-1, keepdims=True)
    byte = np.maximum(np.where(amax > 0, np.frexp(amax)[1] - 1 + 127, 0) - down, 1)
    scale = np.exp2(byte - 127.0)
    codes = (blocks / scale).astype(np.float32).astype(dtype).astype(np.float64)
    return np.moveaxis((codes * scale).reshape(v.shape), -1, axis)


WIDE = False


def mx_kscale(k):
    if not WIDE:
        return np.ones(k)
    levels = np.array([10, -10, 5, -5, 0])
    if k % 512:
        return np.exp2(np.random.permutation(np.resize(levels, k // 32))).repeat(32)
    a = np.empty((k // 512, 16))
    for p in range(k // 512):
        a[p, :8] = np.random.permutation(np.resize(levels, 8))
        for g in range(8):
            far = levels[np.abs(levels - a[p, g]) >= 10]
            a[p, g + 8] = far[np.random.randint(len(far))]
    return np.exp2(a.ravel()).repeat(32)


def f64(x):
    return np.asarray(x).astype(np.float64)


def striped(idx):
    return np.tile(idx.reshape(-1, 16).T, (8, 1)).astype(np.uint16)


def unstriped(offs):
    return offs[:16].T.reshape(-1).astype(np.int64)


def striped8(idx):
    return np.concatenate([x.reshape(-1, 16).T for x in idx]).astype(np.uint16)


def runs(offs, k):
    lists = np.stack([offs[16 * r : 16 * r + 16].T.reshape(-1) for r in range(8)]).astype(np.int64)
    return lists[np.arange(k) % 512 // 64]


def pack_weight(w):
    k, n = w.shape
    w = f64(np.asarray(w, np.float32).astype(ml_dtypes.bfloat16)).reshape(k // 32, 32, n)
    amax = np.abs(w).max(1)
    byte = np.clip(np.where(amax > 0, np.frexp(amax)[1] - 1 + 127 - 7, 1), 1, 254)
    scaled = (w * np.exp2(127.0 - byte)[:, None, :]).reshape(k, n).astype(np.float32)
    words = np.ascontiguousarray(scaled.reshape(k // 512, 128, 4, n).transpose(0, 1, 3, 2)).astype(ml_dtypes.float8_e4m3fn).view(np.uint8)
    return words, np.ascontiguousarray(byte.astype(np.uint8).reshape(k // 512, 16, n))


def unpack_weight(words, scales):
    g, p, n, _ = words.shape
    vals = np.ascontiguousarray(words).view(ml_dtypes.float8_e4m3fn).astype(np.float64) * np.repeat(np.exp2(scales.astype(np.float64) - 127.0), 8, axis=1)[..., None]
    return vals.transpose(0, 1, 3, 2).reshape(g * 512, n)


E2M1 = np.array([0.0, 0.5, 1.0, 1.5, 2.0, 3.0, 4.0, 6.0, -0.0, -0.5, -1.0, -1.5, -2.0, -3.0, -4.0, -6.0])


def pack_fp4(w):
    k, n = w.shape
    w = f64(np.asarray(w, np.float32).astype(ml_dtypes.bfloat16)).reshape(k // 32, 32, n)
    amax = np.abs(w).max(1)
    mant, ex = np.frexp(amax / 6.0)
    byte = np.clip(np.where(amax > 0, np.where(mant > 0.5, ex, ex - 1) + 127, 1), 1, 254)
    scaled = (w * np.exp2(127.0 - byte)[:, None, :]).reshape(k, n).astype(np.float32)
    c = np.ascontiguousarray(scaled.reshape(k // 512, 128, 4, n).transpose(0, 1, 3, 2)).astype(ml_dtypes.float4_e2m1fn).view(np.uint8) & 0xF
    words = (c[..., 0::2] | (c[..., 1::2] << 4)).reshape(k // 512, 128, 2 * n)
    return np.ascontiguousarray(words), np.ascontiguousarray(byte.astype(np.uint8).reshape(k // 512, 16, n))


def unpack_fp4(words, scales):
    g, _, n = scales.shape
    words = np.ascontiguousarray(words).reshape(g, 128, n, 2)
    nib = np.empty((g, 128, n, 4), np.uint8)
    nib[..., 0::2] = words & 0xF
    nib[..., 1::2] = words >> 4
    vals = E2M1[nib] * np.repeat(np.exp2(scales.astype(np.float64) - 127.0), 8, axis=1)[..., None]
    return vals.transpose(0, 1, 3, 2).reshape(g * 512, n)


def planes(y):
    n, m = y.shape
    v = y.astype(np.float32).astype(ml_dtypes.bfloat16).astype(np.float64).reshape(n // 32, 32, m)
    top = np.abs(v).max(1)
    byte = np.clip(np.where(top > 0, np.frexp(top)[1] - 1 + 127 - 7, 1), 1, 254)
    codes = (v * np.exp2(127.0 - byte)[:, None, :]).reshape(n, m).astype(np.float32).astype(ml_dtypes.float8_e4m3fn).view(np.uint8)
    words = codes.reshape(n // 512, 128, 4, m).transpose(0, 1, 3, 2)
    return np.ascontiguousarray(words), np.ascontiguousarray(byte.astype(np.uint8).reshape(n // 512, 16, m))


K, T, S, N, H, W = 512, 2048, 512, 512, 512, 256


def setup_inputs():
    n = np.random.standard_normal
    s = mx_kscale(K)[:, None]
    u = mx_kscale(H)
    packed_xT = pack_weight(n((K, T)) * s)
    packed_w1 = pack_fp4(n((K, H)) / np.sqrt(K) / s)
    packed_w2 = pack_fp4(n((K, H)) / np.sqrt(K) / s)
    packed_w3 = pack_fp4(n((K, H)) / np.sqrt(K) / s)
    packed_w4 = pack_fp4(n((H, N)) / np.sqrt(H) / u[:, None])
    return {
        "x_words": packed_xT[0],
        "x_scales": packed_xT[1],
        "w1_words": packed_w1[0],
        "w1_scales": packed_w1[1],
        "w2_words": packed_w2[0],
        "w2_scales": packed_w2[1],
        "w3_words": packed_w3[0],
        "w3_scales": packed_w3[1],
        "gn": (np.random.uniform(0.5, 1.5, (H, 1)) * u[:, None]).astype(np.float32),
        "w4_words": packed_w4[0],
        "w4_scales": packed_w4[1],
        "offs": striped(np.random.permutation(T)[:S]),
        "two": striped(np.random.permutation(T)[:S]),
        "three": striped(np.random.permutation(T)[:S]),
        "n1": striped8(np.stack([np.random.permutation(S)[:W] for _ in range(8)])),
        "n2": striped8(np.stack([np.random.permutation(S)[:W] for _ in range(8)])),
        "n3": striped8(np.stack([np.random.permutation(S) for _ in range(8)])),
        "n4": striped8(np.stack([np.random.permutation(S) for _ in range(8)])),
        "n5": striped8(np.stack([np.random.permutation(S) for _ in range(8)])),
        "n6": striped8(np.stack([np.random.permutation(S) for _ in range(8)])),
        "n7": striped8(np.stack([np.random.permutation(S) for _ in range(8)])),
    }


def reference(x_words, x_scales, w1_words, w1_scales, w2_words, w2_scales, w3_words, w3_scales, gn, w4_words, w4_scales, offs, two, three, n1, n2, n3, n4, n5, n6, n7):
    x_two = unpack_weight(x_words, x_scales)[:, unstriped(two)]
    d = unpack_fp4(w2_words, w2_scales).T @ x_two
    xq = unpack_weight(x_words, x_scales)[:, unstriped(offs)]
    y = unpack_fp4(w1_words, w1_scales).T @ xq
    ra = d[np.arange(H)[:, None], runs(n2, H)] - (0.5 * (y[np.arange(H)[:, None], runs(n1, H)]))
    m1 = y.copy()
    m1[np.arange(H)[:, None], runs(n1, H)] = ra
    x_three = unpack_weight(x_words, x_scales)[:, unstriped(three)]
    b = unpack_fp4(w3_words, w3_scales).T @ x_three
    z = f64(gn) * (np.maximum(m1[np.arange(H)[:, None], runs(n3, H)] + b[np.arange(H)[:, None], runs(n5, H)], m1[np.arange(H)[:, None], runs(n4, H)] + b[np.arange(H)[:, None], runs(n6, H)]))
    h = unpack_fp4(w4_words, w4_scales).T @ mxq(z, 0, "e4m3")
    pa = h[np.arange(N)[:, None], runs(n7, N)]
    out_0 = (2.0 * (h * pa)) / ((h) ** 2 + (pa) ** 2 + 0.5)
    return (out_0,) + planes(out_0)

@@ -1,0 +1,185 @@
+from contextlib import ExitStack
+
+import concourse.mybir as mybir
+
+K, T, S, N, H, W = 512, 2048, 512, 512, 512, 256
+FLOPS = 4 * 2 * 512 * 512 * 512
+
+F32 = mybir.dt.float32
+BF16 = mybir.dt.bfloat16
+I32 = mybir.dt.int32
+U32 = mybir.dt.uint32
+U16 = mybir.dt.uint16
+U8 = mybir.dt.uint8
+FP8X4 = mybir.dt.float8_e4m3fn_x4
+FP4X4 = mybir.dt.float4_e2m1fn_x4
+ALU = mybir.AluOpType
+ACT = mybir.ActivationFunctionType
+
+P = 128
+PACK = 4
+Z_PIECES = [(0, 256), (256, 384), (384, 512)]
+OUT_PIECES = [(0, 256), (256, 384), (384, 512)]
+
+
+def tile_picked_trioputbpathbharm_none_po_kernel(
+    tc, x_words, x_scales, w1_words, w1_scales, w2_words, w2_scales, w3_words, w3_scales, gn,
+    w4_words, w4_scales, offs, two, three, n1, n2, n3, n4, n5, n6, n7, out_0, out_1, out_2,
+):
+    nc = tc.nc
+    with ExitStack() as ctx:
+        held = ctx.enter_context(tc.tile_pool(name="held", bufs=1))
+        ring = ctx.enter_context(tc.tile_pool(name="ring", bufs=3))
+        psum = ctx.enter_context(tc.psum_pool(name="psum", bufs=1))
+
+        def load_list(name, src):
+            tile = held.tile([P, src.shape[1]], U16, name=name)
+            nc.sync.dma_start(tile[:], src)
+            return tile
+
+        def load_scale_rows(tile, src):
+            for q in range(4):
+                nc.sync.dma_start(tile[32 * q : 32 * q + 4, :].bitcast(I32), src[0, 4 * q : 4 * q + 4, :].bitcast(I32))
+
+        def part(lst, a, b):
+            return lst[:, a // 16 : b // 16]
+
+        xs = held.tile([P, T], U8, name="xs", align_bytes=64)
+        nc.vector.memset(xs[:].bitcast(I32), 0)
+        ws_raw = [held.tile([P, H], U8, name="ws_raw%d" % i, align_bytes=64) for i in range(4)]
+        for i in range(4):
+            nc.vector.memset(ws_raw[i][:].bitcast(I32), 0)
+
+        w_words = [w1_words, w2_words, w3_words, w4_words]
+        w_scales = [w1_scales, w2_scales, w3_scales, w4_scales]
+        ww_raw = [held.tile([P, 2 * H], U8, name="ww_raw%d" % i, align_bytes=64) for i in range(4)]
+        for i in range(4):
+            nc.sync.dma_start(ww_raw[i][:].bitcast(I32), w_words[i][0].bitcast(I32))
+        l_offs = load_list("l_offs", offs)
+        xw = held.tile([P, T], U32, name="xw", align_bytes=64)
+        nc.sync.dma_start(xw[:].bitcast(I32), x_words[0].rearrange("p n t -> p (n t)").bitcast(I32))
+        l_two = load_list("l_two", two)
+        l_three = load_list("l_three", three)
+        load_scale_rows(xs, x_scales)
+        load_scale_rows(ws_raw[0], w_scales[0])
+        load_scale_rows(ws_raw[1], w_scales[1])
+        l1 = load_list("l1", n1)
+        l2 = load_list("l2", n2)
+        load_scale_rows(ws_raw[2], w_scales[2])
+        l3 = load_list("l3", n3)
+        l5 = load_list("l5", n5)
+        l4 = load_list("l4", n4)
+        l6 = load_list("l6", n6)
+        gain = held.tile([P, PACK], F32, name="gain")
+        nc.sync.dma_start(gain[:], gn.rearrange("(p t) o -> p (t o)", t=PACK))
+        load_scale_rows(ws_raw[3], w_scales[3])
+        l7 = load_list("l7", n7)
+
+        ww = [held.tile([P, PACK, 2 * P], U8, name="ww%d" % i, align_bytes=64) for i in range(4)]
+        ws = [held.tile([P, PACK, P], U8, name="ws%d" % i, align_bytes=64) for i in range(4)]
+
+        def deal_words(i):
+            nc.vector.tensor_copy(
+                ww[i][:].rearrange("p t (m e) -> p t m e", e=2),
+                ww_raw[i][:].rearrange("p (m t e) -> p t m e", t=PACK, e=2),
+            )
+
+        def deal_scales(i):
+            nc.vector.tensor_copy(ws[i][:], ws_raw[i][:].rearrange("p (m t) -> p t m", t=PACK))
+
+        def product(i, t, bank, codes, scales):
+            nc.tensor.matmul_mx(
+                out=bank, lhsT=ww[i][:, t, :].bitcast(FP4X4), lhsT_scale=ws[i][:, t, :],
+                rhs=codes.bitcast(FP8X4), rhs_scale=scales, start=True, stop=True,
+            )
+
+        for i in range(4):
+            deal_words(i)
+
+        lists = [l_offs, l_two, l_three]
+        gw = [held.tile([P, S], U32, name="gw%d" % i, align_bytes=64) for i in range(3)]
+        gs = [held.tile([P, S], U8, name="gs%d" % i, align_bytes=64) for i in range(3)]
+        windows = [[held.tile([P, S], F32, name="win%d_%d" % (i, t)) for t in range(PACK)] for i in range(4)]
+        m1, d, b, h = windows
+
+        def project(i):
+            for t in range(PACK):
+                bank = psum.tile([P, S], F32, name="bank%d" % (4 * (i % 2) + t))
+                product(i, t, bank[:], gw[i][:], gs[i][:])
+                nc.scalar.copy(windows[i][t][:], bank[:])
+
+        nc.vector.tensor_copy(gw[0][:], xw[:].indirect(lists[0][:]))
+        nc.vector.tensor_copy(gw[1][:], xw[:].indirect(lists[1][:]))
+        for i in range(2):
+            nc.vector.tensor_copy(gs[i][:], xs[:].indirect(lists[i][:]))
+            deal_scales(i)
+            project(i)
+        nc.vector.tensor_copy(gw[2][:], xw[:].indirect(lists[2][:]))
+        nc.vector.tensor_copy(gs[2][:], xs[:].indirect(lists[2][:]))
+        deal_scales(2)
+        project(2)
+        deal_scales(3)
+
+        ya = held.tile([P, PACK, W], F32, name="ya")
+        da = held.tile([P, PACK, W], F32, name="da")
+        for t in range(PACK):
+            nc.vector.tensor_scalar(ya[:, t, :], m1[t][:].indirect(l1[:]), -0.5, 0.0, ALU.mult, ALU.add)
+        for t in range(PACK):
+            nc.vector.tensor_copy(da[:, t, :], d[t][:].indirect(l2[:]))
+        for t in range(PACK):
+            nc.vector.tensor_tensor(m1[t][:].indirect(l1[:]), da[:, t, :], ya[:, t, :], ALU.add)
+
+        h_bank = [psum.tile([P, S], F32, name="bank%d" % (4 + t)) for t in range(PACK)]
+        hsq = held.tile([P, PACK, S], F32, name="hsq")
+        for (a, e) in Z_PIECES:
+            n = e - a
+            zi = held.tile([P, n, PACK], BF16, name="zi%d" % a, align_bytes=64)
+            for t in range(PACK):
+                g3 = ring.tile([P, n], F32, name="g3")
+                g4 = ring.tile([P, n], F32, name="g4")
+                sa = ring.tile([P, n], F32, name="sa")
+                sb = ring.tile([P, n], F32, name="sb")
+                top = ring.tile([P, n], F32, name="top")
+                nc.vector.tensor_copy(g3[:], m1[t][:].indirect(part(l3, a, e)))
+                nc.vector.tensor_copy(g4[:], m1[t][:].indirect(part(l4, a, e)))
+                nc.vector.tensor_tensor(sa[:], b[t][:].indirect(part(l5, a, e)), g3[:], ALU.add)
+                nc.vector.tensor_tensor(sb[:], b[t][:].indirect(part(l6, a, e)), g4[:], ALU.add)
+                nc.vector.tensor_tensor(top[:], sa[:], sb[:], ALU.max)
+                nc.scalar.activation(zi[:, :, t], top[:], ACT.Copy, scale=gain[:, t : t + 1])
+            zw = held.tile([P, n], U32, name="zw%d" % a, align_bytes=64)
+            zs = held.tile([P, n], U8, name="zs%d" % a, align_bytes=64)
+            nc.vector.quantize_mx(out=zw[:].bitcast(FP8X4), scales=zs[:], in_=zi[:].rearrange("p n t -> p (n t)"))
+            for t in range(PACK):
+                product(3, t, h_bank[t][:, a:e], zw[:], zs[:])
+                nc.scalar.copy(h[t][:, a:e], h_bank[t][:, a:e])
+            for t in range(PACK):
+                nc.scalar.activation(hsq[:, t, a:e], h_bank[t][:, a:e], ACT.Square)
+
+        ow = held.tile([P, S], U32, name="ow", align_bytes=64)
+        osc = held.tile([P, S], U8, name="osc", align_bytes=64)
+        out_rows = out_0.rearrange("(p t) j -> p t j", t=PACK)
+        out_words = out_1[0].rearrange("p n t -> p (n t)").bitcast(I32)
+        for (a, e) in OUT_PIECES:
+            n = e - a
+            res = held.tile([P, PACK, n], F32, name="res%d" % a)
+            for t in range(PACK):
+                pa = ring.tile([P, n], F32, name="pa")
+                pasq = ring.tile([P, n], F32, name="pasq")
+                num = ring.tile([P, n], F32, name="num")
+                den = ring.tile([P, n], F32, name="den")
+                rs = ring.tile([P, n], F32, name="rs")
+                rec = ring.tile([P, n], F32, name="rec")
+                nc.vector.tensor_copy(pa[:], h[t][:].indirect(part(l7, a, e)))
+                nc.scalar.activation(pasq[:], pa[:], ACT.Square)
+                nc.vector.scalar_tensor_tensor(num[:], h_bank[t][:, a:e], 2.0, pa[:], ALU.mult, ALU.mult)
+                nc.vector.tensor_tensor(den[:], pasq[:], hsq[:, t, a:e], ALU.add)
+                nc.scalar.activation(rs[:], den[:], ACT.Abs_reciprocal_sqrt, bias=0.5)
+                nc.scalar.activation(rec[:], rs[:], ACT.Square)
+                nc.vector.tensor_tensor(res[:, t, :], num[:], rec[:], ALU.mult)
+            nc.sync.dma_start(out_rows[:, :, a:e], res[:])
+            oi = held.tile([P, n, PACK], BF16, name="oi%d" % a, align_bytes=64)
+            nc.scalar.copy(oi[:], res[:].rearrange("p t n -> p n t"))
+            nc.vector.quantize_mx(out=ow[:, a:e].bitcast(FP8X4), scales=osc[:, a:e], in_=oi[:].rearrange("p n t -> p (n t)"))
+            nc.sync.dma_start(out_words[:, a:e], ow[:, a:e].bitcast(I32))
+        for q in range(4):
+            nc.sync.dma_start(out_2[0, 4 * q : 4 * q + 4, :].bitcast(I32), osc[32 * q : 32 * q + 4, :].bitcast(I32))

@@ -1,9 +1,13 @@
 from contextlib import ExitStack
 
 import concourse.mybir as mybir
+from concourse.masks import make_identity
 
-K, T, S, N, H, W = 512, 2048, 512, 512, 512, 256
-FLOPS = 4 * 2 * 512 * 512 * 512
+TOKENS = 2048
+COLS = 512
+ROWS = 512
+PUT = 256
+FLOPS = 4 * 2 * 512 * ROWS * COLS
 
 F32 = mybir.dt.float32
 BF16 = mybir.dt.bfloat16
@@ -17,9 +21,13 @@ ALU = mybir.AluOpType
 ACT = mybir.ActivationFunctionType
 
 P = 128
-PACK = 4
-Z_PIECES = [(0, 256), (256, 384), (384, 512)]
-OUT_PIECES = [(0, 256), (256, 384), (384, 512)]
+TILES = 4
+HALF = COLS // 2
+Z_DEPTH = 2
+OUT_DEPTH = 4
+RESULT_LAG = 4
+CODES_LAG = 5
+FIRST_DIRECT = 2
 
 
 def tile_picked_trioputbpathbharm_none_po_kernel(
@@ -29,7 +37,7 @@ def tile_picked_trioputbpathbharm_none_po_kernel(
     nc = tc.nc
     with ExitStack() as ctx:
         held = ctx.enter_context(tc.tile_pool(name="held", bufs=1))
-        ring = ctx.enter_context(tc.tile_pool(name="ring", bufs=3))
+        ring = ctx.enter_context(tc.tile_pool(name="ring", bufs=OUT_DEPTH))
         psum = ctx.enter_context(tc.psum_pool(name="psum", bufs=1))
 
         def load_list(name, src):
@@ -41,145 +49,260 @@ def tile_picked_trioputbpathbharm_none_po_kernel(
             for q in range(4):
                 nc.sync.dma_start(tile[32 * q : 32 * q + 4, :].bitcast(I32), src[0, 4 * q : 4 * q + 4, :].bitcast(I32))
 
-        def part(lst, a, b):
-            return lst[:, a // 16 : b // 16]
+        def columns(half):
+            return slice(half * HALF, (half + 1) * HALF)
 
-        xs = held.tile([P, T], U8, name="xs", align_bytes=64)
-        nc.vector.memset(xs[:].bitcast(I32), 0)
-        ws_raw = [held.tile([P, H], U8, name="ws_raw%d" % i, align_bytes=64) for i in range(4)]
+        def entries(list_tile, half):
+            return list_tile[:, half * HALF // 16 : (half + 1) * HALF // 16]
+
+        def direct(half, t):
+            return half == 1 and t >= FIRST_DIRECT
+
+        x_scale_tile = held.tile([P, TOKENS], U8, name="x_scale_tile", align_bytes=64)
+        nc.vector.memset(x_scale_tile[:].bitcast(I32), 0)
+        raw_scales = [held.tile([P, ROWS], U8, name="raw_scales%d" % i, align_bytes=64) for i in range(4)]
         for i in range(4):
-            nc.vector.memset(ws_raw[i][:].bitcast(I32), 0)
+            nc.vector.memset(raw_scales[i][:].bitcast(I32), 0)
 
         w_words = [w1_words, w2_words, w3_words, w4_words]
         w_scales = [w1_scales, w2_scales, w3_scales, w4_scales]
-        ww_raw = [held.tile([P, 2 * H], U8, name="ww_raw%d" % i, align_bytes=64) for i in range(4)]
+        raw_words = [held.tile([P, 2 * ROWS], U8, name="raw_words%d" % i, align_bytes=64) for i in range(4)]
         for i in range(4):
-            nc.sync.dma_start(ww_raw[i][:].bitcast(I32), w_words[i][0].bitcast(I32))
-        l_offs = load_list("l_offs", offs)
-        xw = held.tile([P, T], U32, name="xw", align_bytes=64)
-        nc.sync.dma_start(xw[:].bitcast(I32), x_words[0].rearrange("p n t -> p (n t)").bitcast(I32))
-        l_two = load_list("l_two", two)
-        l_three = load_list("l_three", three)
-        load_scale_rows(xs, x_scales)
-        load_scale_rows(ws_raw[0], w_scales[0])
-        load_scale_rows(ws_raw[1], w_scales[1])
-        l1 = load_list("l1", n1)
-        l2 = load_list("l2", n2)
-        load_scale_rows(ws_raw[2], w_scales[2])
-        l3 = load_list("l3", n3)
-        l5 = load_list("l5", n5)
-        l4 = load_list("l4", n4)
-        l6 = load_list("l6", n6)
-        gain = held.tile([P, PACK], F32, name="gain")
-        nc.sync.dma_start(gain[:], gn.rearrange("(p t) o -> p (t o)", t=PACK))
-        load_scale_rows(ws_raw[3], w_scales[3])
-        l7 = load_list("l7", n7)
+            nc.sync.dma_start(raw_words[i][:].bitcast(I32), w_words[i][0].bitcast(I32))
+        list_offs = load_list("list_offs", offs)
+        x_word_tile = held.tile([P, TOKENS], U32, name="x_word_tile", align_bytes=64)
+        nc.sync.dma_start(x_word_tile[:].bitcast(I32), x_words[0].rearrange("p n t -> p (n t)").bitcast(I32))
+        list_two = load_list("list_two", two)
+        list_three = load_list("list_three", three)
+        load_scale_rows(raw_scales[0], w_scales[0])
+        load_scale_rows(raw_scales[1], w_scales[1])
+        load_scale_rows(x_scale_tile, x_scales)
+        list1 = load_list("list1", n1)
+        list2 = load_list("list2", n2)
+        load_scale_rows(raw_scales[2], w_scales[2])
+        list3 = load_list("list3", n3)
+        list5 = load_list("list5", n5)
+        list4 = load_list("list4", n4)
+        list6 = load_list("list6", n6)
+        gain = held.tile([P, TILES], F32, name="gain")
+        nc.sync.dma_start(gain[:], gn.rearrange("(p t) o -> p (t o)", t=TILES))
+        load_scale_rows(raw_scales[3], w_scales[3])
+        list7 = load_list("list7", n7)
 
-        ww = [held.tile([P, PACK, 2 * P], U8, name="ww%d" % i, align_bytes=64) for i in range(4)]
-        ws = [held.tile([P, PACK, P], U8, name="ws%d" % i, align_bytes=64) for i in range(4)]
+        warm = held.tile([P, 2], F32, name="warm")
+        nc.vector.memset(warm[:, 0:1], 1.0)
+        nc.scalar.activation(warm[:, 1:2], warm[:, 0:1], ACT.Abs_reciprocal_sqrt, bias=0.5)
+        ident = held.tile([P, P], F32, name="ident")
+        make_identity(nc, ident[:])
+
+        dealt_words = [held.tile([P, TILES, 2 * P], U8, name="dealt_words%d" % i, align_bytes=64) for i in range(4)]
+        dealt_scales = [held.tile([P, TILES, P], U8, name="dealt_scales%d" % i, align_bytes=64) for i in range(4)]
 
         def deal_words(i):
             nc.vector.tensor_copy(
-                ww[i][:].rearrange("p t (m e) -> p t m e", e=2),
-                ww_raw[i][:].rearrange("p (m t e) -> p t m e", t=PACK, e=2),
+                dealt_words[i][:].rearrange("p t (m e) -> p t m e", e=2),
+                raw_words[i][:].rearrange("p (m t e) -> p t m e", t=TILES, e=2),
             )
 
         def deal_scales(i):
-            nc.vector.tensor_copy(ws[i][:], ws_raw[i][:].rearrange("p (m t) -> p t m", t=PACK))
+            nc.gpsimd.tensor_copy(dealt_scales[i][:], raw_scales[i][:].rearrange("p (m t) -> p t m", t=TILES))
 
         def product(i, t, bank, codes, scales):
             nc.tensor.matmul_mx(
-                out=bank, lhsT=ww[i][:, t, :].bitcast(FP4X4), lhsT_scale=ws[i][:, t, :],
+                out=bank, lhsT=dealt_words[i][:, t, :].bitcast(FP4X4), lhsT_scale=dealt_scales[i][:, t, :],
                 rhs=codes.bitcast(FP8X4), rhs_scale=scales, start=True, stop=True,
             )
 
         for i in range(4):
             deal_words(i)
 
-        lists = [l_offs, l_two, l_three]
-        gw = [held.tile([P, S], U32, name="gw%d" % i, align_bytes=64) for i in range(3)]
-        gs = [held.tile([P, S], U8, name="gs%d" % i, align_bytes=64) for i in range(3)]
-        windows = [[held.tile([P, S], F32, name="win%d_%d" % (i, t)) for t in range(PACK)] for i in range(4)]
-        m1, d, b, h = windows
+        token_lists = [list_offs, list_two, list_three]
+        picked_words = [held.tile([P, COLS], U32, name="picked_words%d" % i, align_bytes=64) for i in range(3)]
+        picked_scales = [held.tile([P, COLS], U8, name="picked_scales%d" % i, align_bytes=64) for i in range(3)]
+        results = [[held.tile([P, COLS], F32, name="result%d_%d" % (i, t)) for t in range(TILES)] for i in range(4)]
+        m1, d, b, h = results
 
-        def project(i):
-            for t in range(PACK):
-                bank = psum.tile([P, S], F32, name="bank%d" % (4 * (i % 2) + t))
-                product(i, t, bank[:], gw[i][:], gs[i][:])
-                nc.scalar.copy(windows[i][t][:], bank[:])
+        def pick_words(i):
+            nc.vector.tensor_copy(picked_words[i][:], x_word_tile[:].indirect(token_lists[i][:]))
 
-        nc.vector.tensor_copy(gw[0][:], xw[:].indirect(lists[0][:]))
-        nc.vector.tensor_copy(gw[1][:], xw[:].indirect(lists[1][:]))
-        for i in range(2):
-            nc.vector.tensor_copy(gs[i][:], xs[:].indirect(lists[i][:]))
+        def pick_scales_and_project(i):
+            nc.vector.tensor_copy(picked_scales[i][:], x_scale_tile[:].indirect(token_lists[i][:]))
             deal_scales(i)
-            project(i)
-        nc.vector.tensor_copy(gw[2][:], xw[:].indirect(lists[2][:]))
-        nc.vector.tensor_copy(gs[2][:], xs[:].indirect(lists[2][:]))
-        deal_scales(2)
-        project(2)
+            for t in range(TILES):
+                bank = psum.tile([P, COLS], F32, name="bank%d" % (TILES * (i % 2) + t))
+                product(i, t, bank[:], picked_words[i][:], picked_scales[i][:])
+                nc.scalar.copy(results[i][t][:], bank[:])
+
+        pick_words(0)
+        pick_words(1)
+        pick_scales_and_project(0)
+        pick_scales_and_project(1)
+        pick_words(2)
+        pick_scales_and_project(2)
         deal_scales(3)
 
-        ya = held.tile([P, PACK, W], F32, name="ya")
-        da = held.tile([P, PACK, W], F32, name="da")
-        for t in range(PACK):
-            nc.vector.tensor_scalar(ya[:, t, :], m1[t][:].indirect(l1[:]), -0.5, 0.0, ALU.mult, ALU.add)
-        for t in range(PACK):
-            nc.vector.tensor_copy(da[:, t, :], d[t][:].indirect(l2[:]))
-        for t in range(PACK):
-            nc.vector.tensor_tensor(m1[t][:].indirect(l1[:]), da[:, t, :], ya[:, t, :], ALU.add)
+        y_part = held.tile([P, TILES, PUT], F32, name="y_part")
+        ra = held.tile([P, TILES, PUT], F32, name="ra")
+        for t in range(TILES):
+            nc.vector.tensor_scalar(y_part[:, t, :], m1[t][:].indirect(list1[:]), -0.5, 0.0, ALU.mult, ALU.add)
+        for t in range(TILES):
+            nc.vector.tensor_tensor(ra[:, t, :], d[t][:].indirect(list2[:]), y_part[:, t, :], ALU.add)
+        for t in range(TILES):
+            nc.vector.tensor_copy(m1[t][:].indirect(list1[:]), ra[:, t, :])
 
-        h_bank = [psum.tile([P, S], F32, name="bank%d" % (4 + t)) for t in range(PACK)]
-        hsq = held.tile([P, PACK, S], F32, name="hsq")
-        for (a, e) in Z_PIECES:
-            n = e - a
-            zi = held.tile([P, n, PACK], BF16, name="zi%d" % a, align_bytes=64)
-            for t in range(PACK):
-                g3 = ring.tile([P, n], F32, name="g3")
-                g4 = ring.tile([P, n], F32, name="g4")
-                sa = ring.tile([P, n], F32, name="sa")
-                sb = ring.tile([P, n], F32, name="sb")
-                top = ring.tile([P, n], F32, name="top")
-                nc.vector.tensor_copy(g3[:], m1[t][:].indirect(part(l3, a, e)))
-                nc.vector.tensor_copy(g4[:], m1[t][:].indirect(part(l4, a, e)))
-                nc.vector.tensor_tensor(sa[:], b[t][:].indirect(part(l5, a, e)), g3[:], ALU.add)
-                nc.vector.tensor_tensor(sb[:], b[t][:].indirect(part(l6, a, e)), g4[:], ALU.add)
-                nc.vector.tensor_tensor(top[:], sa[:], sb[:], ALU.max)
-                nc.scalar.activation(zi[:, :, t], top[:], ACT.Copy, scale=gain[:, t : t + 1])
-            zw = held.tile([P, n], U32, name="zw%d" % a, align_bytes=64)
-            zs = held.tile([P, n], U8, name="zs%d" % a, align_bytes=64)
-            nc.vector.quantize_mx(out=zw[:].bitcast(FP8X4), scales=zs[:], in_=zi[:].rearrange("p n t -> p (n t)"))
-            for t in range(PACK):
-                product(3, t, h_bank[t][:, a:e], zw[:], zs[:])
-                nc.scalar.copy(h[t][:, a:e], h_bank[t][:, a:e])
-            for t in range(PACK):
-                nc.scalar.activation(hsq[:, t, a:e], h_bank[t][:, a:e], ACT.Square)
+        h_bank = [psum.tile([P, COLS], F32, name="bank%d" % (TILES + t)) for t in range(TILES)]
+        h_squared = held.tile([P, TILES, COLS], F32, name="h_squared")
+        z_rounded = [held.tile([P, HALF, TILES], BF16, name="z_rounded%d" % i, align_bytes=64) for i in range(2)]
+        z_words = [held.tile([P, HALF], U32, name="z_words%d" % i, align_bytes=64) for i in range(2)]
+        z_scales = [held.tile([P, HALF], U8, name="z_scales%d" % i, align_bytes=64) for i in range(2)]
 
-        ow = held.tile([P, S], U32, name="ow", align_bytes=64)
-        osc = held.tile([P, S], U8, name="osc", align_bytes=64)
-        out_rows = out_0.rearrange("(p t) j -> p t j", t=PACK)
+        def z_tile(tag):
+            return ring.tile([P, HALF], F32, name=tag, bufs=Z_DEPTH)
+
+        def add_transposed(bank, first, second):
+            for c in range(0, HALF, P):
+                nc.tensor.matmul(bank[:, c : c + P], lhsT=first[:, c : c + P], rhs=ident[:], is_transpose=True, start=True, stop=False)
+                nc.tensor.matmul(bank[:, c : c + P], lhsT=second[:, c : c + P], rhs=ident[:], is_transpose=True, start=False, stop=True)
+
+        def transpose_back(bank, turned):
+            for c in range(0, HALF, P):
+                nc.tensor.transpose(bank[:, c : c + P], turned[:, c : c + P], ident[:])
+
+        def z_by_transposes(half, tiles):
+            m_at_4 = {t: z_tile("z_a") for t in tiles}
+            sum_b = {t: z_tile("z_b") for t in tiles}
+            m_less_b = {t: z_tile("z_c") for t in tiles}
+            excess = {t: z_tile("z_d") for t in tiles}
+            for t in tiles:
+                nc.vector.tensor_copy(m_at_4[t][:], m1[t][:].indirect(entries(list4, half)))
+            for t in tiles:
+                nc.vector.tensor_tensor(sum_b[t][:], b[t][:].indirect(entries(list6, half)), m_at_4[t][:], ALU.add)
+            for t in tiles:
+                nc.vector.tensor_tensor(m_less_b[t][:], m1[t][:].indirect(entries(list3, half)), sum_b[t][:], ALU.subtract)
+            for t in tiles:
+                nc.vector.tensor_tensor(excess[t][:], b[t][:].indirect(entries(list5, half)), m_less_b[t][:], ALU.add)
+            for t in tiles:
+                positive = z_tile("z_e")
+                nc.scalar.activation(positive[:], excess[t][:], ACT.Relu)
+                turned_bank = psum.tile([P, HALF], F32, name="bank%d" % (t % 2))
+                add_transposed(turned_bank, sum_b[t], positive)
+                turned = z_tile("z_f")
+                nc.scalar.copy(turned[:], turned_bank[:])
+                larger_bank = psum.tile([P, HALF], F32, name="bank%d" % (2 + t % 2))
+                transpose_back(larger_bank, turned)
+                nc.scalar.activation(z_rounded[half][:, :, t], larger_bank[:], ACT.Copy, scale=gain[:, t : t + 1])
+
+        def fetch_m1(half, t):
+            m_at_3 = z_tile("z_c")
+            m_at_4 = z_tile("z_a")
+            nc.vector.tensor_copy(m_at_3[:], m1[t][:].indirect(entries(list3, half)))
+            nc.vector.tensor_copy(m_at_4[:], m1[t][:].indirect(entries(list4, half)))
+            return m_at_3, m_at_4
+
+        def add_b(half, t, m_at_3, m_at_4):
+            sum_a = z_tile("z_d")
+            sum_b = z_tile("z_b")
+            nc.vector.tensor_tensor(sum_a[:], b[t][:].indirect(entries(list5, half)), m_at_3[:], ALU.add)
+            nc.vector.tensor_tensor(sum_b[:], b[t][:].indirect(entries(list6, half)), m_at_4[:], ALU.add)
+            return sum_a, sum_b
+
+        def z_on_vector(half, t, sum_a, sum_b):
+            larger = z_tile("z_e")
+            nc.vector.tensor_tensor(larger[:], sum_a[:], sum_b[:], ALU.max)
+            nc.vector.tensor_scalar(z_rounded[half][:, :, t], larger[:], gain[:, t : t + 1], None, ALU.mult)
+
+        def make_h(half):
+            cols = columns(half)
+            nc.vector.quantize_mx(
+                out=z_words[half][:].bitcast(FP8X4), scales=z_scales[half][:], in_=z_rounded[half][:].rearrange("p n t -> p (n t)")
+            )
+            for t in range(TILES):
+                product(3, t, h_bank[t][:, cols], z_words[half][:], z_scales[half][:])
+                nc.scalar.copy(h[t][:, cols], h_bank[t][:, cols])
+            for t in range(TILES):
+                nc.scalar.activation(h_squared[:, t, cols], h[t][:, cols], ACT.Square)
+
+        z_by_transposes(0, (0, 1))
+        z_by_transposes(0, (2, 3))
+        z_by_transposes(1, (0, 1))
+        make_h(0)
+        sums_2 = add_b(1, 2, *fetch_m1(1, 2))
+        fetched_3 = fetch_m1(1, 3)
+        z_on_vector(1, 2, *sums_2)
+        z_on_vector(1, 3, *add_b(1, 3, *fetched_3))
+        make_h(1)
+
+        out_word_tile = held.tile([P, COLS], U32, name="out_word_tile", align_bytes=64)
+        out_scale_tile = held.tile([P, COLS], U8, name="out_scale_tile", align_bytes=64)
+        out_rows = out_0.rearrange("(p t) j -> p t j", t=TILES)
         out_words = out_1[0].rearrange("p n t -> p (n t)").bitcast(I32)
-        for (a, e) in OUT_PIECES:
-            n = e - a
-            res = held.tile([P, PACK, n], F32, name="res%d" % a)
-            for t in range(PACK):
-                pa = ring.tile([P, n], F32, name="pa")
-                pasq = ring.tile([P, n], F32, name="pasq")
-                num = ring.tile([P, n], F32, name="num")
-                den = ring.tile([P, n], F32, name="den")
-                rs = ring.tile([P, n], F32, name="rs")
-                rec = ring.tile([P, n], F32, name="rec")
-                nc.vector.tensor_copy(pa[:], h[t][:].indirect(part(l7, a, e)))
-                nc.scalar.activation(pasq[:], pa[:], ACT.Square)
-                nc.vector.scalar_tensor_tensor(num[:], h_bank[t][:, a:e], 2.0, pa[:], ALU.mult, ALU.mult)
-                nc.vector.tensor_tensor(den[:], pasq[:], hsq[:, t, a:e], ALU.add)
-                nc.scalar.activation(rs[:], den[:], ACT.Abs_reciprocal_sqrt, bias=0.5)
-                nc.scalar.activation(rec[:], rs[:], ACT.Square)
-                nc.vector.tensor_tensor(res[:, t, :], num[:], rec[:], ALU.mult)
-            nc.sync.dma_start(out_rows[:, :, a:e], res[:])
-            oi = held.tile([P, n, PACK], BF16, name="oi%d" % a, align_bytes=64)
-            nc.scalar.copy(oi[:], res[:].rearrange("p t n -> p n t"))
-            nc.vector.quantize_mx(out=ow[:, a:e].bitcast(FP8X4), scales=osc[:, a:e], in_=oi[:].rearrange("p n t -> p (n t)"))
-            nc.sync.dma_start(out_words[:, a:e], ow[:, a:e].bitcast(I32))
+        out_values = [held.tile([P, TILES, HALF], F32, name="out_values%d" % i) for i in range(2)]
+        out_rounded = [held.tile([P, HALF, TILES], BF16, name="out_rounded%d" % i, align_bytes=64) for i in range(2)]
+
+        def out_tile(tag):
+            return ring.tile([P, HALF], F32, name=tag)
+
+        def fetch_pa(half, t):
+            pa = out_tile("pa")
+            pa_squared = out_tile("pa_squared")
+            nc.vector.tensor_copy(pa[:], h[t][:].indirect(entries(list7, half)))
+            nc.scalar.activation(pa_squared[:], pa[:], ACT.Square)
+            return pa, pa_squared
+
+        def factors(half, t, pa, pa_squared):
+            cols = columns(half)
+            h_pa = out_tile("h_pa")
+            root = out_tile("root")
+            r = out_tile("r")
+            if direct(half, t):
+                squares = out_tile("squares")
+                nc.vector.tensor_tensor(squares[:], pa_squared[:], h_squared[:, t, cols], ALU.add)
+                nc.vector.tensor_tensor(h_pa[:], h_bank[t][:, cols], pa[:], ALU.mult)
+            else:
+                squares = psum.tile([P, HALF], F32, name="bank%d" % (t % 2))
+                add_transposed(squares, h_squared[:, t, cols], pa_squared)
+                nc.gpsimd.tensor_tensor(h_pa[:], h[t][:, cols], pa[:], ALU.mult)
+            nc.scalar.activation(root[:], squares[:], ACT.Abs_reciprocal_sqrt, bias=0.25, scale=0.5)
+            nc.scalar.activation(r[:], root[:], ACT.Square)
+            if direct(half, t):
+                return h_pa, r
+            r_bank = psum.tile([P, HALF], F32, name="bank%d" % (2 + t % 2))
+            transpose_back(r_bank, r)
+            return h_pa, r_bank
+
+        def result(half, t, h_pa, r):
+            values, rounded = out_values[half], out_rounded[half]
+            nc.vector.tensor_tensor(values[:, t, :], h_pa[:], r[:], ALU.mult)
+            if t % 2 == 0:
+                return
+            pair = slice(t - 1, t + 1)
+            nc.sync.dma_start(out_rows[:, pair, columns(half)], values[:, pair, :])
+            if half == 1 and t == 1:
+                nc.scalar.copy(rounded[:, :, pair], values[:, pair, :].rearrange("p t n -> p n t"))
+            elif half == 1:
+                nc.vector.tensor_copy(rounded[:, :, pair], values[:, pair, :].rearrange("p t n -> p n t"))
+            elif t == TILES - 1:
+                nc.vector.tensor_copy(rounded[:], values[:].rearrange("p t n -> p n t"))
+
+        def out_codes(half):
+            cols = columns(half)
+            nc.vector.quantize_mx(
+                out=out_word_tile[:, cols].bitcast(FP8X4), scales=out_scale_tile[:, cols],
+                in_=out_rounded[half][:].rearrange("p n t -> p (n t)"),
+            )
+            nc.sync.dma_start(out_words[:, cols], out_word_tile[:, cols].bitcast(I32))
+
+        steps = [(half, t) for half in range(2) for t in range(TILES)]
+        fetched, made = {}, {}
+        for u in range(len(steps) + CODES_LAG):
+            if u < len(steps):
+                fetched[u] = fetch_pa(*steps[u])
+            if 1 <= u <= len(steps):
+                made[u - 1] = factors(*steps[u - 1], *fetched[u - 1])
+            if RESULT_LAG <= u < len(steps) + RESULT_LAG:
+                result(*steps[u - RESULT_LAG], *made[u - RESULT_LAG])
+            if u >= CODES_LAG and steps[u - CODES_LAG][1] == TILES - 1:
+                out_codes(steps[u - CODES_LAG][0])
         for q in range(4):
-            nc.sync.dma_start(out_2[0, 4 * q : 4 * q + 4, :].bitcast(I32), osc[32 * q : 32 * q + 4, :].bitcast(I32))
+            queue = nc.scalar if q % 2 else nc.sync
+            queue.dma_start(out_2[0, 4 * q : 4 * q + 4, :].bitcast(I32), out_scale_tile[32 * q : 32 * q + 4, :].bitcast(I32))

from contextlib import ExitStack

import concourse.mybir as mybir
from concourse.masks import make_identity

TOKENS = 2048
COLS = 512
ROWS = 512
PUT = 256
FLOPS = 4 * 2 * 512 * ROWS * COLS

F32 = mybir.dt.float32
BF16 = mybir.dt.bfloat16
I32 = mybir.dt.int32
U32 = mybir.dt.uint32
U16 = mybir.dt.uint16
U8 = mybir.dt.uint8
FP8X4 = mybir.dt.float8_e4m3fn_x4
FP4X4 = mybir.dt.float4_e2m1fn_x4
ALU = mybir.AluOpType
ACT = mybir.ActivationFunctionType

P = 128
TILES = 4
HALF = COLS // 2
Z_DEPTH = 2
OUT_DEPTH = 4
RESULT_LAG = 4
CODES_LAG = 5
FIRST_DIRECT = 2


def tile_picked_trioputbpathbharm_none_po_kernel(
    tc, x_words, x_scales, w1_words, w1_scales, w2_words, w2_scales, w3_words, w3_scales, gn,
    w4_words, w4_scales, offs, two, three, n1, n2, n3, n4, n5, n6, n7, out_0, out_1, out_2,
):
    nc = tc.nc
    with ExitStack() as ctx:
        held = ctx.enter_context(tc.tile_pool(name="held", bufs=1))
        ring = ctx.enter_context(tc.tile_pool(name="ring", bufs=OUT_DEPTH))
        psum = ctx.enter_context(tc.psum_pool(name="psum", bufs=1))

        def load_list(name, src):
            tile = held.tile([P, src.shape[1]], U16, name=name)
            nc.sync.dma_start(tile[:], src)
            return tile

        def load_scale_rows(tile, src):
            for q in range(4):
                nc.sync.dma_start(tile[32 * q : 32 * q + 4, :].bitcast(I32), src[0, 4 * q : 4 * q + 4, :].bitcast(I32))

        def columns(half):
            return slice(half * HALF, (half + 1) * HALF)

        def entries(list_tile, half):
            return list_tile[:, half * HALF // 16 : (half + 1) * HALF // 16]

        def direct(half, t):
            return half == 1 and t >= FIRST_DIRECT

        x_scale_tile = held.tile([P, TOKENS], U8, name="x_scale_tile", align_bytes=64)
        nc.vector.memset(x_scale_tile[:].bitcast(I32), 0)
        raw_scales = [held.tile([P, ROWS], U8, name="raw_scales%d" % i, align_bytes=64) for i in range(4)]
        for i in range(4):
            nc.vector.memset(raw_scales[i][:].bitcast(I32), 0)

        w_words = [w1_words, w2_words, w3_words, w4_words]
        w_scales = [w1_scales, w2_scales, w3_scales, w4_scales]
        raw_words = [held.tile([P, 2 * ROWS], U8, name="raw_words%d" % i, align_bytes=64) for i in range(4)]
        for i in range(4):
            nc.sync.dma_start(raw_words[i][:].bitcast(I32), w_words[i][0].bitcast(I32))
        list_offs = load_list("list_offs", offs)
        x_word_tile = held.tile([P, TOKENS], U32, name="x_word_tile", align_bytes=64)
        nc.sync.dma_start(x_word_tile[:].bitcast(I32), x_words[0].rearrange("p n t -> p (n t)").bitcast(I32))
        list_two = load_list("list_two", two)
        list_three = load_list("list_three", three)
        load_scale_rows(raw_scales[0], w_scales[0])
        load_scale_rows(raw_scales[1], w_scales[1])
        load_scale_rows(x_scale_tile, x_scales)
        list1 = load_list("list1", n1)
        list2 = load_list("list2", n2)
        load_scale_rows(raw_scales[2], w_scales[2])
        list3 = load_list("list3", n3)
        list5 = load_list("list5", n5)
        list4 = load_list("list4", n4)
        list6 = load_list("list6", n6)
        gain = held.tile([P, TILES], F32, name="gain")
        nc.sync.dma_start(gain[:], gn.rearrange("(p t) o -> p (t o)", t=TILES))
        load_scale_rows(raw_scales[3], w_scales[3])
        list7 = load_list("list7", n7)

        warm = held.tile([P, 2], F32, name="warm")
        nc.vector.memset(warm[:, 0:1], 1.0)
        nc.scalar.activation(warm[:, 1:2], warm[:, 0:1], ACT.Abs_reciprocal_sqrt, bias=0.5)
        ident = held.tile([P, P], F32, name="ident")
        make_identity(nc, ident[:])

        dealt_words = [held.tile([P, TILES, 2 * P], U8, name="dealt_words%d" % i, align_bytes=64) for i in range(4)]
        dealt_scales = [held.tile([P, TILES, P], U8, name="dealt_scales%d" % i, align_bytes=64) for i in range(4)]

        def deal_words(i):
            nc.vector.tensor_copy(
                dealt_words[i][:].rearrange("p t (m e) -> p t m e", e=2),
                raw_words[i][:].rearrange("p (m t e) -> p t m e", t=TILES, e=2),
            )

        def deal_scales(i):
            nc.gpsimd.tensor_copy(dealt_scales[i][:], raw_scales[i][:].rearrange("p (m t) -> p t m", t=TILES))

        def product(i, t, bank, codes, scales):
            nc.tensor.matmul_mx(
                out=bank, lhsT=dealt_words[i][:, t, :].bitcast(FP4X4), lhsT_scale=dealt_scales[i][:, t, :],
                rhs=codes.bitcast(FP8X4), rhs_scale=scales, start=True, stop=True,
            )

        for i in range(4):
            deal_words(i)

        token_lists = [list_offs, list_two, list_three]
        picked_words = [held.tile([P, COLS], U32, name="picked_words%d" % i, align_bytes=64) for i in range(3)]
        picked_scales = [held.tile([P, COLS], U8, name="picked_scales%d" % i, align_bytes=64) for i in range(3)]
        results = [[held.tile([P, COLS], F32, name="result%d_%d" % (i, t)) for t in range(TILES)] for i in range(4)]
        m1, d, b, h = results

        def pick_words(i):
            nc.vector.tensor_copy(picked_words[i][:], x_word_tile[:].indirect(token_lists[i][:]))

        def pick_scales_and_project(i):
            nc.vector.tensor_copy(picked_scales[i][:], x_scale_tile[:].indirect(token_lists[i][:]))
            deal_scales(i)
            for t in range(TILES):
                bank = psum.tile([P, COLS], F32, name="bank%d" % (TILES * (i % 2) + t))
                product(i, t, bank[:], picked_words[i][:], picked_scales[i][:])
                nc.scalar.copy(results[i][t][:], bank[:])

        pick_words(0)
        pick_words(1)
        pick_scales_and_project(0)
        pick_scales_and_project(1)
        pick_words(2)
        pick_scales_and_project(2)
        deal_scales(3)

        y_part = held.tile([P, TILES, PUT], F32, name="y_part")
        ra = held.tile([P, TILES, PUT], F32, name="ra")
        for t in range(TILES):
            nc.vector.tensor_scalar(y_part[:, t, :], m1[t][:].indirect(list1[:]), -0.5, 0.0, ALU.mult, ALU.add)
        for t in range(TILES):
            nc.vector.tensor_tensor(ra[:, t, :], d[t][:].indirect(list2[:]), y_part[:, t, :], ALU.add)
        for t in range(TILES):
            nc.vector.tensor_copy(m1[t][:].indirect(list1[:]), ra[:, t, :])

        h_bank = [psum.tile([P, COLS], F32, name="bank%d" % (TILES + t)) for t in range(TILES)]
        h_squared = held.tile([P, TILES, COLS], F32, name="h_squared")
        z_rounded = [held.tile([P, HALF, TILES], BF16, name="z_rounded%d" % i, align_bytes=64) for i in range(2)]
        z_words = [held.tile([P, HALF], U32, name="z_words%d" % i, align_bytes=64) for i in range(2)]
        z_scales = [held.tile([P, HALF], U8, name="z_scales%d" % i, align_bytes=64) for i in range(2)]

        def z_tile(tag):
            return ring.tile([P, HALF], F32, name=tag, bufs=Z_DEPTH)

        def add_transposed(bank, first, second):
            for c in range(0, HALF, P):
                nc.tensor.matmul(bank[:, c : c + P], lhsT=first[:, c : c + P], rhs=ident[:], is_transpose=True, start=True, stop=False)
                nc.tensor.matmul(bank[:, c : c + P], lhsT=second[:, c : c + P], rhs=ident[:], is_transpose=True, start=False, stop=True)

        def transpose_back(bank, turned):
            for c in range(0, HALF, P):
                nc.tensor.transpose(bank[:, c : c + P], turned[:, c : c + P], ident[:])

        def z_by_transposes(half, tiles):
            m_at_4 = {t: z_tile("z_a") for t in tiles}
            sum_b = {t: z_tile("z_b") for t in tiles}
            m_less_b = {t: z_tile("z_c") for t in tiles}
            excess = {t: z_tile("z_d") for t in tiles}
            for t in tiles:
                nc.vector.tensor_copy(m_at_4[t][:], m1[t][:].indirect(entries(list4, half)))
            for t in tiles:
                nc.vector.tensor_tensor(sum_b[t][:], b[t][:].indirect(entries(list6, half)), m_at_4[t][:], ALU.add)
            for t in tiles:
                nc.vector.tensor_tensor(m_less_b[t][:], m1[t][:].indirect(entries(list3, half)), sum_b[t][:], ALU.subtract)
            for t in tiles:
                nc.vector.tensor_tensor(excess[t][:], b[t][:].indirect(entries(list5, half)), m_less_b[t][:], ALU.add)
            for t in tiles:
                positive = z_tile("z_e")
                nc.scalar.activation(positive[:], excess[t][:], ACT.Relu)
                turned_bank = psum.tile([P, HALF], F32, name="bank%d" % (t % 2))
                add_transposed(turned_bank, sum_b[t], positive)
                turned = z_tile("z_f")
                nc.scalar.copy(turned[:], turned_bank[:])
                larger_bank = psum.tile([P, HALF], F32, name="bank%d" % (2 + t % 2))
                transpose_back(larger_bank, turned)
                nc.scalar.activation(z_rounded[half][:, :, t], larger_bank[:], ACT.Copy, scale=gain[:, t : t + 1])

        def fetch_m1(half, t):
            m_at_3 = z_tile("z_c")
            m_at_4 = z_tile("z_a")
            nc.vector.tensor_copy(m_at_3[:], m1[t][:].indirect(entries(list3, half)))
            nc.vector.tensor_copy(m_at_4[:], m1[t][:].indirect(entries(list4, half)))
            return m_at_3, m_at_4

        def add_b(half, t, m_at_3, m_at_4):
            sum_a = z_tile("z_d")
            sum_b = z_tile("z_b")
            nc.vector.tensor_tensor(sum_a[:], b[t][:].indirect(entries(list5, half)), m_at_3[:], ALU.add)
            nc.vector.tensor_tensor(sum_b[:], b[t][:].indirect(entries(list6, half)), m_at_4[:], ALU.add)
            return sum_a, sum_b

        def z_on_vector(half, t, sum_a, sum_b):
            larger = z_tile("z_e")
            nc.vector.tensor_tensor(larger[:], sum_a[:], sum_b[:], ALU.max)
            nc.vector.tensor_scalar(z_rounded[half][:, :, t], larger[:], gain[:, t : t + 1], None, ALU.mult)

        def make_h(half):
            cols = columns(half)
            nc.vector.quantize_mx(
                out=z_words[half][:].bitcast(FP8X4), scales=z_scales[half][:], in_=z_rounded[half][:].rearrange("p n t -> p (n t)")
            )
            for t in range(TILES):
                product(3, t, h_bank[t][:, cols], z_words[half][:], z_scales[half][:])
                nc.scalar.copy(h[t][:, cols], h_bank[t][:, cols])
            for t in range(TILES):
                nc.scalar.activation(h_squared[:, t, cols], h[t][:, cols], ACT.Square)

        z_by_transposes(0, (0, 1))
        z_by_transposes(0, (2, 3))
        z_by_transposes(1, (0, 1))
        make_h(0)
        sums_2 = add_b(1, 2, *fetch_m1(1, 2))
        fetched_3 = fetch_m1(1, 3)
        z_on_vector(1, 2, *sums_2)
        z_on_vector(1, 3, *add_b(1, 3, *fetched_3))
        make_h(1)

        out_word_tile = held.tile([P, COLS], U32, name="out_word_tile", align_bytes=64)
        out_scale_tile = held.tile([P, COLS], U8, name="out_scale_tile", align_bytes=64)
        out_rows = out_0.rearrange("(p t) j -> p t j", t=TILES)
        out_words = out_1[0].rearrange("p n t -> p (n t)").bitcast(I32)
        out_values = [held.tile([P, TILES, HALF], F32, name="out_values%d" % i) for i in range(2)]
        out_rounded = [held.tile([P, HALF, TILES], BF16, name="out_rounded%d" % i, align_bytes=64) for i in range(2)]

        def out_tile(tag):
            return ring.tile([P, HALF], F32, name=tag)

        def fetch_pa(half, t):
            pa = out_tile("pa")
            pa_squared = out_tile("pa_squared")
            nc.vector.tensor_copy(pa[:], h[t][:].indirect(entries(list7, half)))
            nc.scalar.activation(pa_squared[:], pa[:], ACT.Square)
            return pa, pa_squared

        def factors(half, t, pa, pa_squared):
            cols = columns(half)
            h_pa = out_tile("h_pa")
            root = out_tile("root")
            r = out_tile("r")
            if direct(half, t):
                squares = out_tile("squares")
                nc.vector.tensor_tensor(squares[:], pa_squared[:], h_squared[:, t, cols], ALU.add)
                nc.vector.tensor_tensor(h_pa[:], h_bank[t][:, cols], pa[:], ALU.mult)
            else:
                squares = psum.tile([P, HALF], F32, name="bank%d" % (t % 2))
                add_transposed(squares, h_squared[:, t, cols], pa_squared)
                nc.gpsimd.tensor_tensor(h_pa[:], h[t][:, cols], pa[:], ALU.mult)
            nc.scalar.activation(root[:], squares[:], ACT.Abs_reciprocal_sqrt, bias=0.25, scale=0.5)
            nc.scalar.activation(r[:], root[:], ACT.Square)
            if direct(half, t):
                return h_pa, r
            r_bank = psum.tile([P, HALF], F32, name="bank%d" % (2 + t % 2))
            transpose_back(r_bank, r)
            return h_pa, r_bank

        def result(half, t, h_pa, r):
            values, rounded = out_values[half], out_rounded[half]
            nc.vector.tensor_tensor(values[:, t, :], h_pa[:], r[:], ALU.mult)
            if t % 2 == 0:
                return
            pair = slice(t - 1, t + 1)
            nc.sync.dma_start(out_rows[:, pair, columns(half)], values[:, pair, :])
            if half == 1 and t == 1:
                nc.scalar.copy(rounded[:, :, pair], values[:, pair, :].rearrange("p t n -> p n t"))
            elif half == 1:
                nc.vector.tensor_copy(rounded[:, :, pair], values[:, pair, :].rearrange("p t n -> p n t"))
            elif t == TILES - 1:
                nc.vector.tensor_copy(rounded[:], values[:].rearrange("p t n -> p n t"))

        def out_codes(half):
            cols = columns(half)
            nc.vector.quantize_mx(
                out=out_word_tile[:, cols].bitcast(FP8X4), scales=out_scale_tile[:, cols],
                in_=out_rounded[half][:].rearrange("p n t -> p (n t)"),
            )
            nc.sync.dma_start(out_words[:, cols], out_word_tile[:, cols].bitcast(I32))

        steps = [(half, t) for half in range(2) for t in range(TILES)]
        fetched, made = {}, {}
        for u in range(len(steps) + CODES_LAG):
            if u < len(steps):
                fetched[u] = fetch_pa(*steps[u])
            if 1 <= u <= len(steps):
                made[u - 1] = factors(*steps[u - 1], *fetched[u - 1])
            if RESULT_LAG <= u < len(steps) + RESULT_LAG:
                result(*steps[u - RESULT_LAG], *made[u - RESULT_LAG])
            if u >= CODES_LAG and steps[u - CODES_LAG][1] == TILES - 1:
                out_codes(steps[u - CODES_LAG][0])
        for q in range(4):
            queue = nc.scalar if q % 2 else nc.sync
            queue.dma_start(out_2[0, 4 * q : 4 * q + 4, :].bitcast(I32), out_scale_tile[32 * q : 32 * q + 4, :].bitcast(I32))
